import numpy as np
import ml_dtypes


def mxq(x, axis, fmt="e4m3"):
    dtype, down = {"e4m3": (ml_dtypes.float8_e4m3fn, 7), "e5m2": (ml_dtypes.float8_e5m2, 14)}[fmt]
    v = np.moveaxis(np.asarray(x, np.float32).astype(ml_dtypes.bfloat16).astype(np.float64), axis, -1)
    blocks = v.reshape(v.shape[:-1] + (-1, 32))
    amax = np.abs(blocks).max(-1, keepdims=True)
    byte = np.maximum(np.where(amax > 0, np.frexp(amax)[1] - 1 + 127, 0) - down, 1)
    scale = np.exp2(byte - 127.0)
    codes = (blocks / scale).astype(np.float32).astype(dtype).astype(np.float64)
    return np.moveaxis((codes * scale).reshape(v.shape), -1, axis)


WIDE = False


def mx_kscale(k):
    if not WIDE:
        return np.ones(k)
    levels = np.array([10, -10, 5, -5, 0])
    if k % 512:
        return np.exp2(np.random.permutation(np.resize(levels, k // 32))).repeat(32)
    a = np.empty((k // 512, 16))
    for p in range(k // 512):
        a[p, :8] = np.random.permutation(np.resize(levels, 8))
        for g in range(8):
            far = levels[np.abs(levels - a[p, g]) >= 10]
            a[p, g + 8] = far[np.random.randint(len(far))]
    return np.exp2(a.ravel()).repeat(32)


def f64(x):
    return np.asarray(x).astype(np.float64)


def striped(idx):
    return np.tile(np.asarray(idx).reshape(-1, 16).T, (8, 1)).astype(np.uint16)


def unstriped(offs):
    return offs[:16].T.reshape(-1).astype(np.int64)


E2M1 = np.array([0.0, 0.5, 1.0, 1.5, 2.0, 3.0, 4.0, 6.0, -0.0, -0.5, -1.0, -1.5, -2.0, -3.0, -4.0, -6.0])


def pack_weight(w, fmt):
    k, n = w.shape
    w = f64(np.asarray(w, np.float32).astype(ml_dtypes.bfloat16)).reshape(k // 32, 32, n)
    amax = np.abs(w).max(1)
    if fmt == "e4m3":
        byte = np.frexp(amax)[1] - 1 + 127 - 7
    else:
        mant, ex = np.frexp(amax / 6.0)
        byte = np.where(mant > 0.5, ex, ex - 1) + 127
    byte = np.clip(np.where(amax > 0, byte, 1), 1, 254)
    scaled = (w * np.exp2(127.0 - byte)[:, None, :]).reshape(k, n).astype(np.float32)
    by_word = np.ascontiguousarray(scaled.reshape(k // 512, 128, 4, n).transpose(0, 1, 3, 2))
    if fmt == "e4m3":
        words = by_word.astype(ml_dtypes.float8_e4m3fn).view(np.uint8)
    else:
        c = by_word.astype(ml_dtypes.float4_e2m1fn).view(np.uint8) & 0xF
        words = (c[..., 0::2] | (c[..., 1::2] << 4)).reshape(k // 512, 128, 2 * n)
    return np.ascontiguousarray(words), np.ascontiguousarray(byte.astype(np.uint8).reshape(k // 512, 16, n))


def unpack_weight(words, scales, fmt):
    g, _, n = scales.shape
    words = np.ascontiguousarray(words).reshape(g, 128, n, -1)
    if fmt == "e4m3":
        vals = words.view(ml_dtypes.float8_e4m3fn).astype(np.float64)
    else:
        nib = np.empty((g, 128, n, 4), np.uint8)
        nib[..., 0::2] = words & 0xF
        nib[..., 1::2] = words >> 4
        vals = E2M1[nib]
    vals = vals * np.repeat(np.exp2(scales.astype(np.float64) - 127.0), 8, axis=1)[..., None]
    return vals.transpose(0, 1, 3, 2).reshape(g * 512, n)


D, E, T, I, Q = 512, 512, 2048, 512, 128


def setup_inputs():
    n = np.random.standard_normal
    idx = np.random.permutation(T)[:I]
    fd = mx_kscale(D)
    fe = mx_kscale(E)
    keysp = pack_weight(n((D, T)) / fd[:, None], "e2m1")
    valsp = pack_weight(n((E, T)) / fe[:, None], "e2m1")
    return {
        "query": (n((D, Q)) * 1.0 / np.sqrt(D) * fd[:, None]).astype(np.float32),
        "keys_words": keysp[0],
        "keys_scales": keysp[1],
        "floor": (np.random.uniform(0.05, 0.3, (Q, 1))).astype(np.float32),
        "reserve": (np.random.uniform(20.0, 100.0, (Q, 1))).astype(np.float32),
        "gout": (n((E, Q)) * 1 / np.sqrt(E) * fe[:, None]).astype(np.float32),
        "vals_words": valsp[0],
        "vals_scales": valsp[1],
        "dquery": (n((D, Q)) * 1.0 / np.sqrt(D) * fd[:, None]).astype(np.float32),
        "base": (0.5 * n((Q, T))).astype(np.float32),
        "offs": striped(idx),
    }


def reference(query, keys_words, keys_scales, floor, reserve, gout, vals_words, vals_scales, dquery, base, offs):
    idx = unstriped(offs)
    keysu = unpack_weight(keys_words, keys_scales, "e2m1")
    valsu = unpack_weight(vals_words, vals_scales, "e2m1")
    queryq = mxq(f64(query), 0, "e4m3")
    keysidxg = keysu[:, idx]
    a = queryq.T @ keysidxg
    dqueryq = mxq(f64(dquery), 0, "e4m3")
    ta = dqueryq.T @ keysidxg
    p = np.square(a) + f64(floor)
    z = np.sum(p, axis=1, keepdims=True) + f64(reserve)
    goutq = mxq(f64(gout), 0, "e4m3")
    valsidxg = valsu[:, idx]
    c0 = goutq.T @ valsidxg
    dz = np.sum(c0 * p / np.square(z) * (-1.0), axis=1, keepdims=True)
    dp = c0 / z + dz
    tp = ta * a * 2.0
    tz = np.sum(tp, axis=1, keepdims=True)
    tdz = np.sum((tp * c0 - tz * z * 2.0 * c0 * p / np.square(z)) / np.square(z) * (-1.0), axis=1, keepdims=True)
    tdp = tz * c0 / np.square(z) * (-1.0) + tdz
    tda = (tdp * a + ta * dp) * 2.0
    gs = tda * 512.0
    gf = np.zeros((Q, T))
    gf[:, idx] = gs
    y = f64(base) + gf
    return y

@@ -1,0 +1,142 @@
+from contextlib import ExitStack
+
+import concourse.mybir as mybir
+
+F32 = mybir.dt.float32
+BF16 = mybir.dt.bfloat16
+I32 = mybir.dt.int32
+U32 = mybir.dt.uint32
+U16 = mybir.dt.uint16
+U8 = mybir.dt.uint8
+FP8X4 = mybir.dt.float8_e4m3fn_x4
+FP4X4 = mybir.dt.float4_e2m1fn_x4
+ADD = mybir.AluOpType.add
+MULT = mybir.AluOpType.mult
+SUB = mybir.AluOpType.subtract
+ACT = mybir.ActivationFunctionType
+
+P = 128
+K = 512
+T = 2048
+SLOTS = 512
+Q = 128
+PARTS = 2
+CHUNKS = [256,512,512,512,256]
+FLOPS = 3 * 2 * K * Q * SLOTS
+
+
+def tile_attend_hvsquareshares_s_kernel(tc, query, keys_words, keys_scales, floor, reserve, gout, vals_words, vals_scales, dquery, base, offs, out):
+    nc = tc.nc
+    with ExitStack() as ctx:
+        sb = ctx.enter_context(tc.tile_pool(name="sb", bufs=1))
+        ps = ctx.enter_context(tc.psum_pool(name="ps", bufs=1))
+
+        offsets = sb.tile([P, SLOTS // 16], U16, name="offsets")
+        k_words = sb.tile([P, T], U16, name="k_words", align_bytes=64)
+        v_words = sb.tile([P, T], U16, name="v_words", tag="vals_then_tp", align_bytes=64)
+        k_bytes = sb.tile([P, T], U8, name="k_bytes", align_bytes=64)
+        v_bytes = sb.tile([P, T], U8, name="v_bytes", align_bytes=64)
+        window = sb.tile([P, T], F32, name="window", align_bytes=64)
+        floor_sb = sb.tile([P, 1], F32, name="floor_sb")
+        reserve_sb = sb.tile([P, 1], F32, name="reserve_sb")
+        raw_q = sb.tile([P, 4, Q], F32, name="raw_q", align_bytes=64)
+        raw_d = sb.tile([P, 4, Q], F32, name="raw_d", align_bytes=64)
+        raw_g = sb.tile([P, 4, Q], F32, name="raw_g", tag="gout_then_base", align_bytes=64)
+
+        def load_bytes(tile, scales):
+            for r in range(4):
+                nc.sync.dma_start(out=tile[r:P:32, :].bitcast(I32), in_=scales[0, r:16:4, :].bitcast(I32))
+
+        def load_rows(tile, rows):
+            nc.sync.dma_start(out=tile[:], in_=rows.rearrange("(p j) w -> p j w", j=4))
+
+        nc.vector.memset(k_bytes[:].bitcast(I32), 0)
+        nc.vector.memset(v_bytes[:].bitcast(I32), 0)
+        nc.gpsimd.dma_start(out=floor_sb[:], in_=floor)
+        nc.gpsimd.dma_start(out=reserve_sb[:], in_=reserve)
+        nc.sync.dma_start(offsets[:], offs)
+        nc.sync.dma_start(out=k_words[:].bitcast(I32), in_=keys_words[0].bitcast(I32))
+        load_bytes(k_bytes, keys_scales)
+        load_rows(raw_q, query)
+        load_rows(raw_d, dquery)
+        load_bytes(v_bytes, vals_scales)
+        nc.sync.dma_start(out=v_words[:].bitcast(I32), in_=vals_words[0].bitcast(I32))
+        load_rows(raw_g, gout)
+        nc.gpsimd.memset(window[:], 0.0)
+
+        def interleave(dst, raw):
+            nc.scalar.activation(out=dst.rearrange("p (c i t) -> p c t i", i=4, t=4), in_=raw[:].rearrange("p t (c i) -> p c t i", i=4), func=ACT.Copy)
+
+        qd_bf = sb.tile([P, 2 * 4 * Q], BF16, name="qd_bf", tag="qd_then_vb", align_bytes=64)
+        g_bf = sb.tile([P, 4 * Q], BF16, name="g_bf", align_bytes=64)
+        qd_codes = sb.tile([P, 2 * Q], U32, name="qd_codes", align_bytes=64)
+        qd_scale = sb.tile([P, 2 * Q], U8, name="qd_scale", align_bytes=64)
+        g_codes = sb.tile([P, Q], U32, name="g_codes", align_bytes=64)
+        g_scale = sb.tile([P, Q], U8, name="g_scale", align_bytes=64)
+        interleave(qd_bf[:, 0 : 4 * Q], raw_q)
+        interleave(qd_bf[:, 4 * Q : 8 * Q], raw_d)
+        interleave(g_bf[:], raw_g)
+        base_sb = sb.tile([P, T], F32, name="base_sb", tag="gout_then_base", align_bytes=64)
+        nc.sync.dma_start(out=base_sb[:], in_=base)
+
+        kw = sb.tile([P, SLOTS], U16, name="kw", tag="words", align_bytes=64)
+        kb = sb.tile([P, SLOTS], U8, name="kb", align_bytes=64)
+        nc.vector.tensor_copy(kb[:], k_bytes[:].indirect(offsets[:]))
+        nc.vector.tensor_copy(kw[:], k_words[:].indirect(offsets[:]))
+        nc.vector.quantize_mx(out=qd_codes[:].bitcast(FP8X4), scales=qd_scale[:], in_=qd_bf[:])
+
+        a_ps = ps.tile([P, SLOTS], F32, name="a_ps")
+        ta_ps = ps.tile([P, SLOTS], F32, name="ta_ps")
+        nc.tensor.matmul_mx(out=a_ps[:], lhsT=qd_codes[:, 0:Q].bitcast(FP8X4), lhsT_scale=qd_scale[:, 0:Q], rhs=kw[:].bitcast(FP4X4), rhs_scale=kb[:], start=True, stop=True)
+        nc.tensor.matmul_mx(out=ta_ps[:], lhsT=qd_codes[:, Q : 2 * Q].bitcast(FP8X4), lhsT_scale=qd_scale[:, Q : 2 * Q], rhs=kw[:].bitcast(FP4X4), rhs_scale=kb[:], start=True, stop=True)
+
+        vb = sb.tile([P, SLOTS], U8, name="vb", tag="qd_then_vb", align_bytes=64)
+        nc.vector.tensor_copy(vb[:], v_bytes[:].indirect(offsets[:]))
+        nc.vector.quantize_mx(out=g_codes[:].bitcast(FP8X4), scales=g_scale[:], in_=g_bf[:])
+
+        def col(name, tag=None):
+            return sb.tile([P, 1], F32, name=name, tag=tag or name, align_bytes=64)
+
+        def wide(name, tag=None):
+            return sb.tile([P, SLOTS], F32, name=name, tag=tag or name, align_bytes=64)
+
+        z_rest, a2_sum, z, r = col("z_rest"), col("a2_sum", "sum_then_ta"), col("z", "z_then_tz"), col("r")
+        a2, p = wide("a2"), wide("p")
+        nc.gpsimd.tensor_scalar(out=z_rest[:], in0=floor_sb[:], scalar1=float(SLOTS), scalar2=reserve_sb[:], op0=MULT, op1=ADD)
+        nc.scalar.activation(out=a2[:], in_=a_ps[:], func=ACT.Square, accum_out=a2_sum[:])
+        nc.scalar.activation(out=z[:], in_=a2_sum[:], func=ACT.Identity, bias=z_rest[:])
+        ta = wide("ta", "sum_then_ta")
+        nc.scalar.activation(out=ta[:], in_=ta_ps[:], func=ACT.Copy, scale=1024.0)
+        nc.vector.reciprocal(out=r[:], in_=z[:])
+        nc.scalar.activation(out=p[:], in_=a2[:], func=ACT.Identity, bias=floor_sb[:])
+
+        c0 = wide("c0")
+        vw = sb.tile([P, SLOTS], U16, name="vw", tag="words", align_bytes=64)
+        width = SLOTS // PARTS
+        for h in range(PARTS):
+            cols = slice(h * width, (h + 1) * width)
+            c_ps = ps.tile([P, width], F32, name="c_ps%d" % h)
+            nc.vector.tensor_copy(vw[:, cols], v_words[:].indirect(offsets[:, h * width // 16 : (h + 1) * width // 16]))
+            nc.tensor.matmul_mx(out=c_ps[:], lhsT=g_codes[:].bitcast(FP8X4), lhsT_scale=g_scale[:], rhs=vw[:, cols].bitcast(FP4X4), rhs_scale=vb[:, cols], start=True, stop=True)
+            nc.scalar.activation(out=c0[:, cols], in_=c_ps[:], func=ACT.Identity, scale=r[:])
+
+        neg_tz, slope, slope2, e_sum, f_sum, g_sum = col("neg_tz", "z_then_tz"), col("slope"), col("slope2"), col("e_sum"), col("f_sum"), col("g_sum")
+        neg_tp, etmp, ftmp, u0, w1, w2 = wide("neg_tp", "vals_then_tp"), wide("etmp"), wide("ftmp"), wide("u0"), wide("w1"), wide("w2")
+        nc.vector.scalar_tensor_tensor(out=neg_tp[:], in0=a_ps[:], scalar=-2.0, in1=ta[:], op0=MULT, op1=MULT, accum_out=neg_tz[:])
+        nc.scalar.activation(out=slope[:], in_=neg_tz[:], func=ACT.Identity, scale=r[:])
+        nc.scalar.activation(out=slope2[:], in_=slope[:], func=ACT.Copy, scale=-2.0)
+        nc.scalar.activation(out=u0[:], in_=c0[:], func=ACT.Identity, scale=slope[:])
+        nc.vector.scalar_tensor_tensor(out=etmp[:], in0=c0[:], scalar=r[:], in1=p[:], op0=MULT, op1=MULT, accum_out=e_sum[:])
+        nc.vector.scalar_tensor_tensor(out=ftmp[:], in0=c0[:], scalar=r[:], in1=neg_tp[:], op0=MULT, op1=MULT, accum_out=f_sum[:])
+        nc.scalar.activation(out=g_sum[:], in_=e_sum[:], func=ACT.Identity, scale=slope2[:], bias=f_sum[:])
+        nc.vector.scalar_tensor_tensor(out=w2[:], in0=c0[:], scalar=e_sum[:], in1=ta[:], op0=SUB, op1=MULT)
+        nc.vector.scalar_tensor_tensor(out=w1[:], in0=u0[:], scalar=g_sum[:], in1=a_ps[:], op0=ADD, op1=MULT)
+        nc.vector.tensor_tensor(window[:].indirect(offsets[:]), w1[:], w2[:], ADD)
+
+        start = 0
+        for j, n in enumerate(CHUNKS):
+            cols = slice(start, start + n)
+            res = sb.tile([P, n], F32, name="res%d" % j, align_bytes=64)
+            nc.vector.tensor_tensor(res[:], window[:, cols], base_sb[:, cols], ADD)
+            (nc.sync if j % 2 == 0 else nc.scalar).dma_start(out=out[:, cols], in_=res[:])
+            start += n

@@ -33,9 +33,9 @@ def tile_attend_hvsquareshares_s_kernel(tc, query, keys_words, keys_scales, floo
 
         offsets = sb.tile([P, SLOTS // 16], U16, name="offsets")
         k_words = sb.tile([P, T], U16, name="k_words", align_bytes=64)
-        v_words = sb.tile([P, T], U16, name="v_words", tag="vals_then_tp", align_bytes=64)
+        v_words = sb.tile([P, T], U16, name="v_words", align_bytes=64)
         k_bytes = sb.tile([P, T], U8, name="k_bytes", align_bytes=64)
-        v_bytes = sb.tile([P, T], U8, name="v_bytes", align_bytes=64)
+        v_bytes = sb.tile([P, T], U8, name="v_bytes", tag="vals_then_tp", align_bytes=64)
         window = sb.tile([P, T], F32, name="window", align_bytes=64)
         floor_sb = sb.tile([P, 1], F32, name="floor_sb")
         reserve_sb = sb.tile([P, 1], F32, name="reserve_sb")
@@ -58,41 +58,46 @@ def tile_attend_hvsquareshares_s_kernel(tc, query, keys_words, keys_scales, floo
         nc.sync.dma_start(out=k_words[:].bitcast(I32), in_=keys_words[0].bitcast(I32))
         load_bytes(k_bytes, keys_scales)
         load_rows(raw_q, query)
-        load_rows(raw_d, dquery)
-        load_bytes(v_bytes, vals_scales)
         nc.sync.dma_start(out=v_words[:].bitcast(I32), in_=vals_words[0].bitcast(I32))
+        load_rows(raw_d, dquery)
         load_rows(raw_g, gout)
-        nc.gpsimd.memset(window[:], 0.0)
+        load_bytes(v_bytes, vals_scales)
+        nc.vector.memset(window[:].bitcast(I32), 0)
 
         def interleave(dst, raw):
             nc.scalar.activation(out=dst.rearrange("p (c i t) -> p c t i", i=4, t=4), in_=raw[:].rearrange("p t (c i) -> p c t i", i=4), func=ACT.Copy)
 
-        qd_bf = sb.tile([P, 2 * 4 * Q], BF16, name="qd_bf", tag="qd_then_vb", align_bytes=64)
-        g_bf = sb.tile([P, 4 * Q], BF16, name="g_bf", align_bytes=64)
-        qd_codes = sb.tile([P, 2 * Q], U32, name="qd_codes", align_bytes=64)
-        qd_scale = sb.tile([P, 2 * Q], U8, name="qd_scale", align_bytes=64)
-        g_codes = sb.tile([P, Q], U32, name="g_codes", align_bytes=64)
-        g_scale = sb.tile([P, Q], U8, name="g_scale", align_bytes=64)
-        interleave(qd_bf[:, 0 : 4 * Q], raw_q)
-        interleave(qd_bf[:, 4 * Q : 8 * Q], raw_d)
-        interleave(g_bf[:], raw_g)
-        base_sb = sb.tile([P, T], F32, name="base_sb", tag="gout_then_base", align_bytes=64)
-        nc.sync.dma_start(out=base_sb[:], in_=base)
+        def operand(name, n, tag=None):
+            grouped = sb.tile([P, 4 * n], BF16, name=name + "_bf", tag=tag or name + "_bf", align_bytes=64)
+            codes = sb.tile([P, n], U32, name=name + "_codes", align_bytes=64)
+            scale = sb.tile([P, n], U8, name=name + "_scale", align_bytes=64)
+            return grouped, codes, scale
 
-        kw = sb.tile([P, SLOTS], U16, name="kw", tag="words", align_bytes=64)
+        def quantize(op):
+            nc.vector.quantize_mx(out=op[1][:].bitcast(FP8X4), scales=op[2][:], in_=op[0][:])
+
+        def product(dst, op, first, words, scales):
+            nc.tensor.matmul_mx(out=dst, lhsT=op[1][:, first : first + Q].bitcast(FP8X4), lhsT_scale=op[2][:, first : first + Q], rhs=words.bitcast(FP4X4), rhs_scale=scales, start=True, stop=True)
+
+        q_op, dg_op = operand("q", Q, "q_then_vb"), operand("dg", 2 * Q)
+        kw = sb.tile([P, SLOTS], U16, name="kw", align_bytes=64)
         kb = sb.tile([P, SLOTS], U8, name="kb", align_bytes=64)
-        nc.vector.tensor_copy(kb[:], k_bytes[:].indirect(offsets[:]))
-        nc.vector.tensor_copy(kw[:], k_words[:].indirect(offsets[:]))
-        nc.vector.quantize_mx(out=qd_codes[:].bitcast(FP8X4), scales=qd_scale[:], in_=qd_bf[:])
-
+        vb = sb.tile([P, SLOTS], U8, name="vb", align_bytes=64)
         a_ps = ps.tile([P, SLOTS], F32, name="a_ps")
         ta_ps = ps.tile([P, SLOTS], F32, name="ta_ps")
-        nc.tensor.matmul_mx(out=a_ps[:], lhsT=qd_codes[:, 0:Q].bitcast(FP8X4), lhsT_scale=qd_scale[:, 0:Q], rhs=kw[:].bitcast(FP4X4), rhs_scale=kb[:], start=True, stop=True)
-        nc.tensor.matmul_mx(out=ta_ps[:], lhsT=qd_codes[:, Q : 2 * Q].bitcast(FP8X4), lhsT_scale=qd_scale[:, Q : 2 * Q], rhs=kw[:].bitcast(FP4X4), rhs_scale=kb[:], start=True, stop=True)
-
-        vb = sb.tile([P, SLOTS], U8, name="vb", tag="qd_then_vb", align_bytes=64)
-        nc.vector.tensor_copy(vb[:], v_bytes[:].indirect(offsets[:]))
-        nc.vector.quantize_mx(out=g_codes[:].bitcast(FP8X4), scales=g_scale[:], in_=g_bf[:])
+        interleave(q_op[0][:], raw_q)
+        nc.vector.tensor_copy(kw[:], k_words[:].indirect(offsets[:]))
+        nc.vector.tensor_copy(kb[:], k_bytes[:].indirect(offsets[:]))
+        quantize(q_op)
+        product(a_ps[:], q_op, 0, kw[:], kb[:])
+        vw = sb.tile([P, SLOTS], U16, name="vw", tag="q_then_vb", align_bytes=64)
+        nc.vector.tensor_copy(vw[:], v_words[:].indirect(offsets[:]))
+        interleave(dg_op[0][:, 0 : 4 * Q], raw_d)
+        interleave(dg_op[0][:, 4 * Q : 8 * Q], raw_g)
+        base_sb = sb.tile([P, T], F32, name="base_sb", tag="gout_then_base", align_bytes=64)
+        nc.sync.dma_start(out=base_sb[:], in_=base)
+        quantize(dg_op)
+        product(ta_ps[:], dg_op, 0, kw[:], kb[:])
 
         def col(name, tag=None):
             return sb.tile([P, 1], F32, name=name, tag=tag or name, align_bytes=64)
@@ -100,37 +105,42 @@ def tile_attend_hvsquareshares_s_kernel(tc, query, keys_words, keys_scales, floo
         def wide(name, tag=None):
             return sb.tile([P, SLOTS], F32, name=name, tag=tag or name, align_bytes=64)
 
-        z_rest, a2_sum, z, r = col("z_rest"), col("a2_sum", "sum_then_ta"), col("z", "z_then_tz"), col("r")
-        a2, p = wide("a2"), wide("p")
-        nc.gpsimd.tensor_scalar(out=z_rest[:], in0=floor_sb[:], scalar1=float(SLOTS), scalar2=reserve_sb[:], op0=MULT, op1=ADD)
-        nc.scalar.activation(out=a2[:], in_=a_ps[:], func=ACT.Square, accum_out=a2_sum[:])
-        nc.scalar.activation(out=z[:], in_=a2_sum[:], func=ACT.Identity, bias=z_rest[:])
-        ta = wide("ta", "sum_then_ta")
-        nc.scalar.activation(out=ta[:], in_=ta_ps[:], func=ACT.Copy, scale=1024.0)
-        nc.vector.reciprocal(out=r[:], in_=z[:])
-        nc.scalar.activation(out=p[:], in_=a2[:], func=ACT.Identity, bias=floor_sb[:])
+        floor_s, rest, rest_s, a2_sum, z = col("floor_s"), col("rest"), col("rest_s"), col("a2_sum", "sum_then_a"), col("z", "z_then_tz")
+        a2 = wide("a2")
+        nc.gpsimd.tensor_scalar(out=rest[:], in0=floor_sb[:], scalar1=float(SLOTS), scalar2=reserve_sb[:], op0=MULT, op1=ADD)
+        nc.gpsimd.tensor_scalar(out=rest_s[:], in0=rest[:], scalar1=1.0 / 1024, scalar2=0.0, op0=MULT, op1=ADD)
+        nc.gpsimd.tensor_scalar(out=floor_s[:], in0=floor_sb[:], scalar1=1.0 / 1024, scalar2=0.0, op0=MULT, op1=ADD)
+        nc.scalar.activation(out=a2[:], in_=a_ps[:], func=ACT.Square, scale=1.0 / 32, accum_out=a2_sum[:])
+        nc.scalar.activation(out=z[:], in_=a2_sum[:], func=ACT.Identity, bias=rest_s[:])
+        a = wide("a", "sum_then_a")
+        nc.scalar.copy(out=a[:], in_=a_ps[:])
 
         c0 = wide("c0")
-        vw = sb.tile([P, SLOTS], U16, name="vw", tag="words", align_bytes=64)
         width = SLOTS // PARTS
+        banks = []
         for h in range(PARTS):
             cols = slice(h * width, (h + 1) * width)
             c_ps = ps.tile([P, width], F32, name="c_ps%d" % h)
-            nc.vector.tensor_copy(vw[:, cols], v_words[:].indirect(offsets[:, h * width // 16 : (h + 1) * width // 16]))
-            nc.tensor.matmul_mx(out=c_ps[:], lhsT=g_codes[:].bitcast(FP8X4), lhsT_scale=g_scale[:], rhs=vw[:, cols].bitcast(FP4X4), rhs_scale=vb[:, cols], start=True, stop=True)
+            nc.vector.tensor_copy(vb[:, cols], v_bytes[:].indirect(offsets[:, h * width // 16 : (h + 1) * width // 16]))
+            product(c_ps[:], dg_op, Q, vw[:, cols], vb[:, cols])
+            banks.append((cols, c_ps))
+        r = col("r", "vals_then_tp")
+        nc.vector.reciprocal(out=r[:], in_=z[:])
+        for cols, c_ps in banks:
             nc.scalar.activation(out=c0[:, cols], in_=c_ps[:], func=ACT.Identity, scale=r[:])
 
-        neg_tz, slope, slope2, e_sum, f_sum, g_sum = col("neg_tz", "z_then_tz"), col("slope"), col("slope2"), col("e_sum"), col("f_sum"), col("g_sum")
-        neg_tp, etmp, ftmp, u0, w1, w2 = wide("neg_tp", "vals_then_tp"), wide("etmp"), wide("ftmp"), wide("u0"), wide("w1"), wide("w2")
-        nc.vector.scalar_tensor_tensor(out=neg_tp[:], in0=a_ps[:], scalar=-2.0, in1=ta[:], op0=MULT, op1=MULT, accum_out=neg_tz[:])
+        neg_tz, slope, slope2, e_raw, e_sum, f_sum, g_sum = col("neg_tz", "z_then_tz"), col("slope"), col("slope2"), col("e_raw"), col("e_sum"), col("f_sum"), col("g_sum")
+        neg_tp, etmp, ftmp, u0, w1, w2 = wide("neg_tp"), wide("etmp"), wide("ftmp"), wide("u0"), wide("w1"), wide("w2")
+        nc.vector.scalar_tensor_tensor(out=neg_tp[:], in0=ta_ps[:], scalar=-2.0 / 1024, in1=a[:], op0=MULT, op1=MULT, accum_out=neg_tz[:])
         nc.scalar.activation(out=slope[:], in_=neg_tz[:], func=ACT.Identity, scale=r[:])
         nc.scalar.activation(out=slope2[:], in_=slope[:], func=ACT.Copy, scale=-2.0)
+        nc.vector.scalar_tensor_tensor(out=etmp[:], in0=a2[:], scalar=floor_s[:], in1=c0[:], op0=ADD, op1=MULT, accum_out=e_raw[:])
+        nc.scalar.activation(out=e_sum[:], in_=e_raw[:], func=ACT.Identity, scale=r[:])
         nc.scalar.activation(out=u0[:], in_=c0[:], func=ACT.Identity, scale=slope[:])
-        nc.vector.scalar_tensor_tensor(out=etmp[:], in0=c0[:], scalar=r[:], in1=p[:], op0=MULT, op1=MULT, accum_out=e_sum[:])
         nc.vector.scalar_tensor_tensor(out=ftmp[:], in0=c0[:], scalar=r[:], in1=neg_tp[:], op0=MULT, op1=MULT, accum_out=f_sum[:])
         nc.scalar.activation(out=g_sum[:], in_=e_sum[:], func=ACT.Identity, scale=slope2[:], bias=f_sum[:])
-        nc.vector.scalar_tensor_tensor(out=w2[:], in0=c0[:], scalar=e_sum[:], in1=ta[:], op0=SUB, op1=MULT)
-        nc.vector.scalar_tensor_tensor(out=w1[:], in0=u0[:], scalar=g_sum[:], in1=a_ps[:], op0=ADD, op1=MULT)
+        nc.vector.scalar_tensor_tensor(out=w2[:], in0=c0[:], scalar=e_sum[:], in1=ta_ps[:], op0=SUB, op1=MULT)
+        nc.vector.scalar_tensor_tensor(out=w1[:], in0=u0[:], scalar=g_sum[:], in1=a[:], op0=ADD, op1=MULT)
         nc.vector.tensor_tensor(window[:].indirect(offsets[:]), w1[:], w2[:], ADD)
 
         start = 0

@@ -105,15 +105,13 @@ def tile_attend_hvsquareshares_s_kernel(tc, query, keys_words, keys_scales, floo
         def wide(name, tag=None):
             return sb.tile([P, SLOTS], F32, name=name, tag=tag or name, align_bytes=64)
 
-        floor_s, rest, rest_s, a2_sum, z = col("floor_s"), col("rest"), col("rest_s"), col("a2_sum", "sum_then_a"), col("z", "z_then_tz")
+        a2_sum, p_sum, z = col("a2_sum"), col("p_sum", "sum_then_ta"), col("z", "z_then_tz")
         a2 = wide("a2")
-        nc.gpsimd.tensor_scalar(out=rest[:], in0=floor_sb[:], scalar1=float(SLOTS), scalar2=reserve_sb[:], op0=MULT, op1=ADD)
-        nc.gpsimd.tensor_scalar(out=rest_s[:], in0=rest[:], scalar1=1.0 / 1024, scalar2=0.0, op0=MULT, op1=ADD)
-        nc.gpsimd.tensor_scalar(out=floor_s[:], in0=floor_sb[:], scalar1=1.0 / 1024, scalar2=0.0, op0=MULT, op1=ADD)
-        nc.scalar.activation(out=a2[:], in_=a_ps[:], func=ACT.Square, scale=1.0 / 32, accum_out=a2_sum[:])
-        nc.scalar.activation(out=z[:], in_=a2_sum[:], func=ACT.Identity, bias=rest_s[:])
-        a = wide("a", "sum_then_a")
-        nc.scalar.copy(out=a[:], in_=a_ps[:])
+        nc.scalar.activation(out=a2[:], in_=a_ps[:], func=ACT.Square, accum_out=a2_sum[:])
+        nc.scalar.activation(out=p_sum[:], in_=floor_sb[:], func=ACT.Identity, scale=float(SLOTS), bias=a2_sum[:])
+        nc.scalar.activation(out=z[:], in_=reserve_sb[:], func=ACT.Identity, bias=p_sum[:])
+        ta = wide("ta", "sum_then_ta")
+        nc.scalar.activation(out=ta[:], in_=ta_ps[:], func=ACT.Copy, scale=1024.0)
 
         c0 = wide("c0")
         width = SLOTS // PARTS
@@ -131,16 +129,16 @@ def tile_attend_hvsquareshares_s_kernel(tc, query, keys_words, keys_scales, floo
 
         neg_tz, slope, slope2, e_raw, e_sum, f_sum, g_sum = col("neg_tz", "z_then_tz"), col("slope"), col("slope2"), col("e_raw"), col("e_sum"), col("f_sum"), col("g_sum")
         neg_tp, etmp, ftmp, u0, w1, w2 = wide("neg_tp"), wide("etmp"), wide("ftmp"), wide("u0"), wide("w1"), wide("w2")
-        nc.vector.scalar_tensor_tensor(out=neg_tp[:], in0=ta_ps[:], scalar=-2.0 / 1024, in1=a[:], op0=MULT, op1=MULT, accum_out=neg_tz[:])
+        nc.vector.scalar_tensor_tensor(out=neg_tp[:], in0=a_ps[:], scalar=-2.0, in1=ta[:], op0=MULT, op1=MULT, accum_out=neg_tz[:])
         nc.scalar.activation(out=slope[:], in_=neg_tz[:], func=ACT.Identity, scale=r[:])
         nc.scalar.activation(out=slope2[:], in_=slope[:], func=ACT.Copy, scale=-2.0)
-        nc.vector.scalar_tensor_tensor(out=etmp[:], in0=a2[:], scalar=floor_s[:], in1=c0[:], op0=ADD, op1=MULT, accum_out=e_raw[:])
+        nc.vector.scalar_tensor_tensor(out=etmp[:], in0=a2[:], scalar=floor_sb[:], in1=c0[:], op0=ADD, op1=MULT, accum_out=e_raw[:])
         nc.scalar.activation(out=e_sum[:], in_=e_raw[:], func=ACT.Identity, scale=r[:])
         nc.scalar.activation(out=u0[:], in_=c0[:], func=ACT.Identity, scale=slope[:])
         nc.vector.scalar_tensor_tensor(out=ftmp[:], in0=c0[:], scalar=r[:], in1=neg_tp[:], op0=MULT, op1=MULT, accum_out=f_sum[:])
         nc.scalar.activation(out=g_sum[:], in_=e_sum[:], func=ACT.Identity, scale=slope2[:], bias=f_sum[:])
-        nc.vector.scalar_tensor_tensor(out=w2[:], in0=c0[:], scalar=e_sum[:], in1=ta_ps[:], op0=SUB, op1=MULT)
-        nc.vector.scalar_tensor_tensor(out=w1[:], in0=u0[:], scalar=g_sum[:], in1=a[:], op0=ADD, op1=MULT)
+        nc.vector.scalar_tensor_tensor(out=w2[:], in0=c0[:], scalar=e_sum[:], in1=ta[:], op0=SUB, op1=MULT)
+        nc.vector.scalar_tensor_tensor(out=w1[:], in0=u0[:], scalar=g_sum[:], in1=a_ps[:], op0=ADD, op1=MULT)
         nc.vector.tensor_tensor(window[:].indirect(offsets[:]), w1[:], w2[:], ADD)
 
         start = 0

@@ -33,9 +33,9 @@ def tile_attend_hvsquareshares_s_kernel(tc, query, keys_words, keys_scales, floo
 
         offsets = sb.tile([P, SLOTS // 16], U16, name="offsets")
         k_words = sb.tile([P, T], U16, name="k_words", align_bytes=64)
-        v_words = sb.tile([P, T], U16, name="v_words", align_bytes=64)
+        v_words = sb.tile([P, T], U16, name="v_words", tag="vals_then_tp", align_bytes=64)
         k_bytes = sb.tile([P, T], U8, name="k_bytes", align_bytes=64)
-        v_bytes = sb.tile([P, T], U8, name="v_bytes", tag="vals_then_tp", align_bytes=64)
+        v_bytes = sb.tile([P, T], U8, name="v_bytes", align_bytes=64)
         window = sb.tile([P, T], F32, name="window", align_bytes=64)
         floor_sb = sb.tile([P, 1], F32, name="floor_sb")
         reserve_sb = sb.tile([P, 1], F32, name="reserve_sb")
@@ -44,8 +44,7 @@ def tile_attend_hvsquareshares_s_kernel(tc, query, keys_words, keys_scales, floo
         raw_g = sb.tile([P, 4, Q], F32, name="raw_g", tag="gout_then_base", align_bytes=64)
 
         def load_bytes(tile, scales):
-            for r in range(4):
-                nc.sync.dma_start(out=tile[r:P:32, :].bitcast(I32), in_=scales[0, r:16:4, :].bitcast(I32))
+            nc.sync.dma_start(out=tile[0:P:8, :].bitcast(I32), in_=scales[0].bitcast(I32))
 
         def load_rows(tile, rows):
             nc.sync.dma_start(out=tile[:], in_=rows.rearrange("(p j) w -> p j w", j=4))
@@ -55,13 +54,13 @@ def tile_attend_hvsquareshares_s_kernel(tc, query, keys_words, keys_scales, floo
         nc.gpsimd.dma_start(out=floor_sb[:], in_=floor)
         nc.gpsimd.dma_start(out=reserve_sb[:], in_=reserve)
         nc.sync.dma_start(offsets[:], offs)
-        nc.sync.dma_start(out=k_words[:].bitcast(I32), in_=keys_words[0].bitcast(I32))
-        load_bytes(k_bytes, keys_scales)
         load_rows(raw_q, query)
+        load_bytes(k_bytes, keys_scales)
+        load_bytes(v_bytes, vals_scales)
+        nc.sync.dma_start(out=k_words[:].bitcast(I32), in_=keys_words[0].bitcast(I32))
         nc.sync.dma_start(out=v_words[:].bitcast(I32), in_=vals_words[0].bitcast(I32))
         load_rows(raw_d, dquery)
         load_rows(raw_g, gout)
-        load_bytes(v_bytes, vals_scales)
         nc.vector.memset(window[:].bitcast(I32), 0)
 
         def interleave(dst, raw):
@@ -79,19 +78,25 @@ def tile_attend_hvsquareshares_s_kernel(tc, query, keys_words, keys_scales, floo
         def product(dst, op, first, words, scales):
             nc.tensor.matmul_mx(out=dst, lhsT=op[1][:, first : first + Q].bitcast(FP8X4), lhsT_scale=op[2][:, first : first + Q], rhs=words.bitcast(FP4X4), rhs_scale=scales, start=True, stop=True)
 
-        q_op, dg_op = operand("q", Q, "q_then_vb"), operand("dg", 2 * Q)
+        def gather_scales(name, table):
+            picked = sb.tile([P, SLOTS], U8, name=name + "_picked", align_bytes=64)
+            plane = sb.tile([P, SLOTS], U8, name=name + "_plane", align_bytes=64)
+            nc.vector.tensor_copy(picked[:], table[:].indirect(offsets[:]))
+            nc.vector.memset(plane[:].bitcast(I32), 0)
+            for r in range(4):
+                nc.sync.dma_start(out=plane[r:P:32, :].bitcast(I32), in_=picked[8 * r : P : 32, :].bitcast(I32))
+            return plane
+
+        q_op, dg_op = operand("q", Q), operand("dg", 2 * Q, "dg_then_vw")
         kw = sb.tile([P, SLOTS], U16, name="kw", align_bytes=64)
-        kb = sb.tile([P, SLOTS], U8, name="kb", align_bytes=64)
-        vb = sb.tile([P, SLOTS], U8, name="vb", align_bytes=64)
         a_ps = ps.tile([P, SLOTS], F32, name="a_ps")
         ta_ps = ps.tile([P, SLOTS], F32, name="ta_ps")
         interleave(q_op[0][:], raw_q)
-        nc.vector.tensor_copy(kw[:], k_words[:].indirect(offsets[:]))
-        nc.vector.tensor_copy(kb[:], k_bytes[:].indirect(offsets[:]))
+        kb = gather_scales("kb", k_bytes)
+        vb = gather_scales("vb", v_bytes)
         quantize(q_op)
+        nc.vector.tensor_copy(kw[:], k_words[:].indirect(offsets[:]))
         product(a_ps[:], q_op, 0, kw[:], kb[:])
-        vw = sb.tile([P, SLOTS], U16, name="vw", tag="q_then_vb", align_bytes=64)
-        nc.vector.tensor_copy(vw[:], v_words[:].indirect(offsets[:]))
         interleave(dg_op[0][:, 0 : 4 * Q], raw_d)
         interleave(dg_op[0][:, 4 * Q : 8 * Q], raw_g)
         base_sb = sb.tile([P, T], F32, name="base_sb", tag="gout_then_base", align_bytes=64)
@@ -105,11 +110,11 @@ def tile_attend_hvsquareshares_s_kernel(tc, query, keys_words, keys_scales, floo
         def wide(name, tag=None):
             return sb.tile([P, SLOTS], F32, name=name, tag=tag or name, align_bytes=64)
 
-        a2_sum, p_sum, z = col("a2_sum"), col("p_sum", "sum_then_ta"), col("z", "z_then_tz")
+        rest, a2_sum, z = col("rest"), col("a2_sum", "sum_then_ta"), col("z", "z_then_tz")
         a2 = wide("a2")
+        nc.gpsimd.tensor_scalar(out=rest[:], in0=floor_sb[:], scalar1=float(SLOTS), scalar2=reserve_sb[:], op0=MULT, op1=ADD)
         nc.scalar.activation(out=a2[:], in_=a_ps[:], func=ACT.Square, accum_out=a2_sum[:])
-        nc.scalar.activation(out=p_sum[:], in_=floor_sb[:], func=ACT.Identity, scale=float(SLOTS), bias=a2_sum[:])
-        nc.scalar.activation(out=z[:], in_=reserve_sb[:], func=ACT.Identity, bias=p_sum[:])
+        nc.scalar.activation(out=z[:], in_=a2_sum[:], func=ACT.Identity, bias=rest[:])
         ta = wide("ta", "sum_then_ta")
         nc.scalar.activation(out=ta[:], in_=ta_ps[:], func=ACT.Copy, scale=1024.0)
 
@@ -119,8 +124,9 @@ def tile_attend_hvsquareshares_s_kernel(tc, query, keys_words, keys_scales, floo
         for h in range(PARTS):
             cols = slice(h * width, (h + 1) * width)
             c_ps = ps.tile([P, width], F32, name="c_ps%d" % h)
-            nc.vector.tensor_copy(vb[:, cols], v_bytes[:].indirect(offsets[:, h * width // 16 : (h + 1) * width // 16]))
-            product(c_ps[:], dg_op, Q, vw[:, cols], vb[:, cols])
+            vw = sb.tile([P, width], U16, name="vw%d" % h, tag="dg_then_vw" if h == PARTS - 1 else "vw%d" % h, align_bytes=64)
+            nc.vector.tensor_copy(vw[:], v_words[:].indirect(offsets[:, h * width // 16 : (h + 1) * width // 16]))
+            product(c_ps[:], dg_op, Q, vw[:], vb[:, cols])
             banks.append((cols, c_ps))
         r = col("r", "vals_then_tp")
         nc.vector.reciprocal(out=r[:], in_=z[:])

@@ -16,38 +16,48 @@ SUB = mybir.AluOpType.subtract
 ACT = mybir.ActivationFunctionType
 
 P = 128
-K = 512
+PACK = 4
+K = P * PACK
 T = 2048
 SLOTS = 512
 Q = 128
-PARTS = 2
-CHUNKS = [256,512,512,512,256]
+LIST_ROWS = 16
+QUADRANT = 32
+BLOCK_PARTITIONS = 8
+GAIN = 1024.0
+HALF = SLOTS // 2
+STORE_WIDTHS = [256, 512, 512, 512, 256]
 FLOPS = 3 * 2 * K * Q * SLOTS
 
 
-def tile_attend_hvsquareshares_s_kernel(tc, query, keys_words, keys_scales, floor, reserve, gout, vals_words, vals_scales, dquery, base, offs, out):
+def tile_attend_hvsquareshares_s_kernel(
+    tc, query, keys_words, keys_scales, floor, reserve, gout, vals_words, vals_scales, dquery, base, offs, out
+):
     nc = tc.nc
     with ExitStack() as ctx:
         sb = ctx.enter_context(tc.tile_pool(name="sb", bufs=1))
         ps = ctx.enter_context(tc.psum_pool(name="ps", bufs=1))
 
-        offsets = sb.tile([P, SLOTS // 16], U16, name="offsets")
+        offsets = sb.tile([P, SLOTS // LIST_ROWS], U16, name="offsets")
         k_words = sb.tile([P, T], U16, name="k_words", align_bytes=64)
-        v_words = sb.tile([P, T], U16, name="v_words", tag="vals_then_tp", align_bytes=64)
+        v_words = sb.tile([P, T], U16, name="v_words", tag="v_words_then_r", align_bytes=64)
         k_bytes = sb.tile([P, T], U8, name="k_bytes", align_bytes=64)
         v_bytes = sb.tile([P, T], U8, name="v_bytes", align_bytes=64)
         window = sb.tile([P, T], F32, name="window", align_bytes=64)
         floor_sb = sb.tile([P, 1], F32, name="floor_sb")
         reserve_sb = sb.tile([P, 1], F32, name="reserve_sb")
-        raw_q = sb.tile([P, 4, Q], F32, name="raw_q", align_bytes=64)
-        raw_d = sb.tile([P, 4, Q], F32, name="raw_d", align_bytes=64)
-        raw_g = sb.tile([P, 4, Q], F32, name="raw_g", tag="gout_then_base", align_bytes=64)
+        raw_q = sb.tile([P, PACK, Q], F32, name="raw_q", align_bytes=64)
+        raw_d = sb.tile([P, PACK, Q], F32, name="raw_d", align_bytes=64)
+        raw_g = sb.tile([P, PACK, Q], F32, name="raw_g", tag="gout_then_base", align_bytes=64)
 
         def load_bytes(tile, scales):
-            nc.sync.dma_start(out=tile[0:P:8, :].bitcast(I32), in_=scales[0].bitcast(I32))
+            nc.sync.dma_start(out=tile[0:P:BLOCK_PARTITIONS, :].bitcast(I32), in_=scales[0].bitcast(I32))
+
+        def load_words(tile, words):
+            nc.sync.dma_start(out=tile[:].bitcast(I32), in_=words[0].bitcast(I32))
 
         def load_rows(tile, rows):
-            nc.sync.dma_start(out=tile[:], in_=rows.rearrange("(p j) w -> p j w", j=4))
+            nc.sync.dma_start(out=tile[:], in_=rows.rearrange("(p j) w -> p j w", j=PACK))
 
         nc.vector.memset(k_bytes[:].bitcast(I32), 0)
         nc.vector.memset(v_bytes[:].bitcast(I32), 0)
@@ -57,100 +67,128 @@ def tile_attend_hvsquareshares_s_kernel(tc, query, keys_words, keys_scales, floo
         load_rows(raw_q, query)
         load_bytes(k_bytes, keys_scales)
         load_bytes(v_bytes, vals_scales)
-        nc.sync.dma_start(out=k_words[:].bitcast(I32), in_=keys_words[0].bitcast(I32))
-        nc.sync.dma_start(out=v_words[:].bitcast(I32), in_=vals_words[0].bitcast(I32))
+        load_words(k_words, keys_words)
         load_rows(raw_d, dquery)
         load_rows(raw_g, gout)
+        load_words(v_words, vals_words)
         nc.vector.memset(window[:].bitcast(I32), 0)
 
         def interleave(dst, raw):
-            nc.scalar.activation(out=dst.rearrange("p (c i t) -> p c t i", i=4, t=4), in_=raw[:].rearrange("p t (c i) -> p c t i", i=4), func=ACT.Copy)
+            nc.scalar.activation(
+                out=dst.rearrange("p (c i t) -> p c t i", i=4, t=PACK),
+                in_=raw[:].rearrange("p t (c i) -> p c t i", i=4),
+                func=ACT.Copy,
+            )
 
-        def operand(name, n, tag=None):
-            grouped = sb.tile([P, 4 * n], BF16, name=name + "_bf", tag=tag or name + "_bf", align_bytes=64)
-            codes = sb.tile([P, n], U32, name=name + "_codes", align_bytes=64)
-            scale = sb.tile([P, n], U8, name=name + "_scale", align_bytes=64)
-            return grouped, codes, scale
+        def operand(name, columns):
+            grouped = sb.tile([P, PACK * columns], BF16, name=name + "_bf", align_bytes=64)
+            codes = sb.tile([P, columns], U32, name=name + "_codes", align_bytes=64)
+            plane = sb.tile([P, columns], U8, name=name + "_scale", align_bytes=64)
+            return grouped, codes, plane
 
         def quantize(op):
-            nc.vector.quantize_mx(out=op[1][:].bitcast(FP8X4), scales=op[2][:], in_=op[0][:])
+            grouped, codes, plane = op
+            nc.vector.quantize_mx(out=codes[:].bitcast(FP8X4), scales=plane[:], in_=grouped[:])
 
-        def product(dst, op, first, words, scales):
-            nc.tensor.matmul_mx(out=dst, lhsT=op[1][:, first : first + Q].bitcast(FP8X4), lhsT_scale=op[2][:, first : first + Q], rhs=words.bitcast(FP4X4), rhs_scale=scales, start=True, stop=True)
+        def product(dst, op, first, words, words_plane):
+            nc.tensor.matmul_mx(
+                out=dst,
+                lhsT=op[1][:, first : first + Q].bitcast(FP8X4),
+                lhsT_scale=op[2][:, first : first + Q],
+                rhs=words.bitcast(FP4X4),
+                rhs_scale=words_plane,
+                start=True,
+                stop=True,
+            )
 
         def gather_scales(name, table):
             picked = sb.tile([P, SLOTS], U8, name=name + "_picked", align_bytes=64)
             plane = sb.tile([P, SLOTS], U8, name=name + "_plane", align_bytes=64)
             nc.vector.tensor_copy(picked[:], table[:].indirect(offsets[:]))
             nc.vector.memset(plane[:].bitcast(I32), 0)
-            for r in range(4):
-                nc.sync.dma_start(out=plane[r:P:32, :].bitcast(I32), in_=picked[8 * r : P : 32, :].bitcast(I32))
+            for j in range(QUADRANT // BLOCK_PARTITIONS):
+                nc.sync.dma_start(
+                    out=plane[j:P:QUADRANT, :].bitcast(I32),
+                    in_=picked[BLOCK_PARTITIONS * j : P : QUADRANT, :].bitcast(I32),
+                )
             return plane
 
-        q_op, dg_op = operand("q", Q), operand("dg", 2 * Q, "dg_then_vw")
+        def half_of_list(h):
+            return offsets[:, h * HALF // LIST_ROWS : (h + 1) * HALF // LIST_ROWS]
+
+        q_op, dg_op = operand("q", Q), operand("dg", 2 * Q)
         kw = sb.tile([P, SLOTS], U16, name="kw", align_bytes=64)
         a_ps = ps.tile([P, SLOTS], F32, name="a_ps")
         ta_ps = ps.tile([P, SLOTS], F32, name="ta_ps")
         interleave(q_op[0][:], raw_q)
-        kb = gather_scales("kb", k_bytes)
-        vb = gather_scales("vb", v_bytes)
+        k_plane = gather_scales("kb", k_bytes)
+        v_plane = gather_scales("vb", v_bytes)
         quantize(q_op)
-        nc.vector.tensor_copy(kw[:], k_words[:].indirect(offsets[:]))
-        product(a_ps[:], q_op, 0, kw[:], kb[:])
-        interleave(dg_op[0][:, 0 : 4 * Q], raw_d)
-        interleave(dg_op[0][:, 4 * Q : 8 * Q], raw_g)
+        for h in range(2):
+            cols = slice(h * HALF, (h + 1) * HALF)
+            nc.vector.tensor_copy(kw[:, cols], k_words[:].indirect(half_of_list(h)))
+            product(a_ps[:, cols], q_op, 0, kw[:, cols], k_plane[:, cols])
+        interleave(dg_op[0][:, 0 : PACK * Q], raw_d)
+        interleave(dg_op[0][:, PACK * Q : 2 * PACK * Q], raw_g)
         base_sb = sb.tile([P, T], F32, name="base_sb", tag="gout_then_base", align_bytes=64)
         nc.sync.dma_start(out=base_sb[:], in_=base)
         quantize(dg_op)
-        product(ta_ps[:], dg_op, 0, kw[:], kb[:])
+        product(ta_ps[:], dg_op, 0, kw[:], k_plane[:])
 
-        def col(name, tag=None):
+        def per_row(name, tag=None):
             return sb.tile([P, 1], F32, name=name, tag=tag or name, align_bytes=64)
 
-        def wide(name, tag=None):
+        def per_slot(name, tag=None):
             return sb.tile([P, SLOTS], F32, name=name, tag=tag or name, align_bytes=64)
 
-        rest, a2_sum, z = col("rest"), col("a2_sum", "sum_then_ta"), col("z", "z_then_tz")
-        a2 = wide("a2")
+        rest, a2_sum, z = per_row("rest"), per_row("a2_sum", "a2_sum_then_ta"), per_row("z", "z_then_tz")
+        a2 = per_slot("a2")
         nc.gpsimd.tensor_scalar(out=rest[:], in0=floor_sb[:], scalar1=float(SLOTS), scalar2=reserve_sb[:], op0=MULT, op1=ADD)
         nc.scalar.activation(out=a2[:], in_=a_ps[:], func=ACT.Square, accum_out=a2_sum[:])
         nc.scalar.activation(out=z[:], in_=a2_sum[:], func=ACT.Identity, bias=rest[:])
-        ta = wide("ta", "sum_then_ta")
-        nc.scalar.activation(out=ta[:], in_=ta_ps[:], func=ACT.Copy, scale=1024.0)
+        ta = per_slot("ta", "a2_sum_then_ta")
+        nc.scalar.activation(out=ta[:], in_=ta_ps[:], func=ACT.Copy, scale=GAIN)
 
-        c0 = wide("c0")
-        width = SLOTS // PARTS
+        c = per_slot("c")
         banks = []
-        for h in range(PARTS):
-            cols = slice(h * width, (h + 1) * width)
-            c_ps = ps.tile([P, width], F32, name="c_ps%d" % h)
-            vw = sb.tile([P, width], U16, name="vw%d" % h, tag="dg_then_vw" if h == PARTS - 1 else "vw%d" % h, align_bytes=64)
-            nc.vector.tensor_copy(vw[:], v_words[:].indirect(offsets[:, h * width // 16 : (h + 1) * width // 16]))
-            product(c_ps[:], dg_op, Q, vw[:], vb[:, cols])
-            banks.append((cols, c_ps))
-        r = col("r", "vals_then_tp")
+        for h in range(2):
+            cols = slice(h * HALF, (h + 1) * HALF)
+            c0_ps = ps.tile([P, HALF], F32, name="c0_ps%d" % h)
+            vw = sb.tile([P, HALF], U16, name="vw%d" % h, align_bytes=64)
+            nc.vector.tensor_copy(vw[:], v_words[:].indirect(half_of_list(h)))
+            product(c0_ps[:], dg_op, Q, vw[:], v_plane[:, cols])
+            banks.append((cols, c0_ps))
+        r = per_row("r", "v_words_then_r")
         nc.vector.reciprocal(out=r[:], in_=z[:])
-        for cols, c_ps in banks:
-            nc.scalar.activation(out=c0[:, cols], in_=c_ps[:], func=ACT.Identity, scale=r[:])
+        for cols, c0_ps in banks:
+            nc.scalar.activation(out=c[:, cols], in_=c0_ps[:], func=ACT.Identity, scale=r[:])
 
-        neg_tz, slope, slope2, e_raw, e_sum, f_sum, g_sum = col("neg_tz", "z_then_tz"), col("slope"), col("slope2"), col("e_raw"), col("e_sum"), col("f_sum"), col("g_sum")
-        neg_tp, etmp, ftmp, u0, w1, w2 = wide("neg_tp"), wide("etmp"), wide("ftmp"), wide("u0"), wide("w1"), wide("w2")
-        nc.vector.scalar_tensor_tensor(out=neg_tp[:], in0=a_ps[:], scalar=-2.0, in1=ta[:], op0=MULT, op1=MULT, accum_out=neg_tz[:])
+        neg_tz, slope, slope_m2 = per_row("neg_tz", "z_then_tz"), per_row("slope"), per_row("slope_m2")
+        pc_sum, e, f, g = per_row("pc_sum"), per_row("e"), per_row("f"), per_row("g")
+        neg_tp, pc, f_terms = per_slot("neg_tp"), per_slot("pc"), per_slot("f_terms")
+        slope_c, a_part, ta_part = per_slot("slope_c"), per_slot("a_part"), per_slot("ta_part")
+        nc.vector.scalar_tensor_tensor(
+            out=neg_tp[:], in0=a_ps[:], scalar=-2.0, in1=ta[:], op0=MULT, op1=MULT, accum_out=neg_tz[:]
+        )
         nc.scalar.activation(out=slope[:], in_=neg_tz[:], func=ACT.Identity, scale=r[:])
-        nc.scalar.activation(out=slope2[:], in_=slope[:], func=ACT.Copy, scale=-2.0)
-        nc.vector.scalar_tensor_tensor(out=etmp[:], in0=a2[:], scalar=floor_sb[:], in1=c0[:], op0=ADD, op1=MULT, accum_out=e_raw[:])
-        nc.scalar.activation(out=e_sum[:], in_=e_raw[:], func=ACT.Identity, scale=r[:])
-        nc.scalar.activation(out=u0[:], in_=c0[:], func=ACT.Identity, scale=slope[:])
-        nc.vector.scalar_tensor_tensor(out=ftmp[:], in0=c0[:], scalar=r[:], in1=neg_tp[:], op0=MULT, op1=MULT, accum_out=f_sum[:])
-        nc.scalar.activation(out=g_sum[:], in_=e_sum[:], func=ACT.Identity, scale=slope2[:], bias=f_sum[:])
-        nc.vector.scalar_tensor_tensor(out=w2[:], in0=c0[:], scalar=e_sum[:], in1=ta[:], op0=SUB, op1=MULT)
-        nc.vector.scalar_tensor_tensor(out=w1[:], in0=u0[:], scalar=g_sum[:], in1=a_ps[:], op0=ADD, op1=MULT)
-        nc.vector.tensor_tensor(window[:].indirect(offsets[:]), w1[:], w2[:], ADD)
+        nc.scalar.activation(out=slope_m2[:], in_=slope[:], func=ACT.Copy, scale=-2.0)
+        nc.vector.scalar_tensor_tensor(
+            out=pc[:], in0=a2[:], scalar=floor_sb[:], in1=c[:], op0=ADD, op1=MULT, accum_out=pc_sum[:]
+        )
+        nc.scalar.activation(out=e[:], in_=pc_sum[:], func=ACT.Identity, scale=r[:])
+        nc.scalar.activation(out=slope_c[:], in_=c[:], func=ACT.Identity, scale=slope[:])
+        nc.vector.scalar_tensor_tensor(
+            out=f_terms[:], in0=c[:], scalar=r[:], in1=neg_tp[:], op0=MULT, op1=MULT, accum_out=f[:]
+        )
+        nc.scalar.activation(out=g[:], in_=e[:], func=ACT.Identity, scale=slope_m2[:], bias=f[:])
+        nc.vector.scalar_tensor_tensor(out=ta_part[:], in0=c[:], scalar=e[:], in1=ta[:], op0=SUB, op1=MULT)
+        nc.vector.scalar_tensor_tensor(out=a_part[:], in0=slope_c[:], scalar=g[:], in1=a_ps[:], op0=ADD, op1=MULT)
+        nc.vector.tensor_tensor(window[:].indirect(offsets[:]), a_part[:], ta_part[:], ADD)
 
         start = 0
-        for j, n in enumerate(CHUNKS):
-            cols = slice(start, start + n)
-            res = sb.tile([P, n], F32, name="res%d" % j, align_bytes=64)
+        for j, width in enumerate(STORE_WIDTHS):
+            cols = slice(start, start + width)
+            res = sb.tile([P, width], F32, name="res%d" % j, align_bytes=64)
             nc.vector.tensor_tensor(res[:], window[:, cols], base_sb[:, cols], ADD)
             (nc.sync if j % 2 == 0 else nc.scalar).dma_start(out=out[:, cols], in_=res[:])
-            start += n
+            start += width

from contextlib import ExitStack

import concourse.mybir as mybir

F32 = mybir.dt.float32
BF16 = mybir.dt.bfloat16
I32 = mybir.dt.int32
U32 = mybir.dt.uint32
U16 = mybir.dt.uint16
U8 = mybir.dt.uint8
FP8X4 = mybir.dt.float8_e4m3fn_x4
FP4X4 = mybir.dt.float4_e2m1fn_x4
ADD = mybir.AluOpType.add
MULT = mybir.AluOpType.mult
SUB = mybir.AluOpType.subtract
ACT = mybir.ActivationFunctionType

P = 128
PACK = 4
K = P * PACK
T = 2048
SLOTS = 512
Q = 128
LIST_ROWS = 16
QUADRANT = 32
BLOCK_PARTITIONS = 8
GAIN = 1024.0
HALF = SLOTS // 2
STORE_WIDTHS = [256, 512, 512, 512, 256]
FLOPS = 3 * 2 * K * Q * SLOTS


def tile_attend_hvsquareshares_s_kernel(
    tc, query, keys_words, keys_scales, floor, reserve, gout, vals_words, vals_scales, dquery, base, offs, out
):
    nc = tc.nc
    with ExitStack() as ctx:
        sb = ctx.enter_context(tc.tile_pool(name="sb", bufs=1))
        ps = ctx.enter_context(tc.psum_pool(name="ps", bufs=1))

        offsets = sb.tile([P, SLOTS // LIST_ROWS], U16, name="offsets")
        k_words = sb.tile([P, T], U16, name="k_words", align_bytes=64)
        v_words = sb.tile([P, T], U16, name="v_words", tag="v_words_then_r", align_bytes=64)
        k_bytes = sb.tile([P, T], U8, name="k_bytes", align_bytes=64)
        v_bytes = sb.tile([P, T], U8, name="v_bytes", align_bytes=64)
        window = sb.tile([P, T], F32, name="window", align_bytes=64)
        floor_sb = sb.tile([P, 1], F32, name="floor_sb")
        reserve_sb = sb.tile([P, 1], F32, name="reserve_sb")
        raw_q = sb.tile([P, PACK, Q], F32, name="raw_q", align_bytes=64)
        raw_d = sb.tile([P, PACK, Q], F32, name="raw_d", align_bytes=64)
        raw_g = sb.tile([P, PACK, Q], F32, name="raw_g", tag="gout_then_base", align_bytes=64)

        def load_bytes(tile, scales):
            nc.sync.dma_start(out=tile[0:P:BLOCK_PARTITIONS, :].bitcast(I32), in_=scales[0].bitcast(I32))

        def load_words(tile, words):
            nc.sync.dma_start(out=tile[:].bitcast(I32), in_=words[0].bitcast(I32))

        def load_rows(tile, rows):
            nc.sync.dma_start(out=tile[:], in_=rows.rearrange("(p j) w -> p j w", j=PACK))

        nc.vector.memset(k_bytes[:].bitcast(I32), 0)
        nc.vector.memset(v_bytes[:].bitcast(I32), 0)
        nc.gpsimd.dma_start(out=floor_sb[:], in_=floor)
        nc.gpsimd.dma_start(out=reserve_sb[:], in_=reserve)
        nc.sync.dma_start(offsets[:], offs)
        load_rows(raw_q, query)
        load_bytes(k_bytes, keys_scales)
        load_bytes(v_bytes, vals_scales)
        load_words(k_words, keys_words)
        load_rows(raw_d, dquery)
        load_rows(raw_g, gout)
        load_words(v_words, vals_words)
        nc.vector.memset(window[:].bitcast(I32), 0)

        def interleave(dst, raw):
            nc.scalar.activation(
                out=dst.rearrange("p (c i t) -> p c t i", i=4, t=PACK),
                in_=raw[:].rearrange("p t (c i) -> p c t i", i=4),
                func=ACT.Copy,
            )

        def operand(name, columns):
            grouped = sb.tile([P, PACK * columns], BF16, name=name + "_bf", align_bytes=64)
            codes = sb.tile([P, columns], U32, name=name + "_codes", align_bytes=64)
            plane = sb.tile([P, columns], U8, name=name + "_scale", align_bytes=64)
            return grouped, codes, plane

        def quantize(op):
            grouped, codes, plane = op
            nc.vector.quantize_mx(out=codes[:].bitcast(FP8X4), scales=plane[:], in_=grouped[:])

        def product(dst, op, first, words, words_plane):
            nc.tensor.matmul_mx(
                out=dst,
                lhsT=op[1][:, first : first + Q].bitcast(FP8X4),
                lhsT_scale=op[2][:, first : first + Q],
                rhs=words.bitcast(FP4X4),
                rhs_scale=words_plane,
                start=True,
                stop=True,
            )

        def gather_scales(name, table):
            picked = sb.tile([P, SLOTS], U8, name=name + "_picked", align_bytes=64)
            plane = sb.tile([P, SLOTS], U8, name=name + "_plane", align_bytes=64)
            nc.vector.tensor_copy(picked[:], table[:].indirect(offsets[:]))
            nc.vector.memset(plane[:].bitcast(I32), 0)
            for j in range(QUADRANT // BLOCK_PARTITIONS):
                nc.sync.dma_start(
                    out=plane[j:P:QUADRANT, :].bitcast(I32),
                    in_=picked[BLOCK_PARTITIONS * j : P : QUADRANT, :].bitcast(I32),
                )
            return plane

        def half_of_list(h):
            return offsets[:, h * HALF // LIST_ROWS : (h + 1) * HALF // LIST_ROWS]

        q_op, dg_op = operand("q", Q), operand("dg", 2 * Q)
        kw = sb.tile([P, SLOTS], U16, name="kw", align_bytes=64)
        a_ps = ps.tile([P, SLOTS], F32, name="a_ps")
        ta_ps = ps.tile([P, SLOTS], F32, name="ta_ps")
        interleave(q_op[0][:], raw_q)
        k_plane = gather_scales("kb", k_bytes)
        v_plane = gather_scales("vb", v_bytes)
        quantize(q_op)
        for h in range(2):
            cols = slice(h * HALF, (h + 1) * HALF)
            nc.vector.tensor_copy(kw[:, cols], k_words[:].indirect(half_of_list(h)))
            product(a_ps[:, cols], q_op, 0, kw[:, cols], k_plane[:, cols])
        interleave(dg_op[0][:, 0 : PACK * Q], raw_d)
        interleave(dg_op[0][:, PACK * Q : 2 * PACK * Q], raw_g)
        base_sb = sb.tile([P, T], F32, name="base_sb", tag="gout_then_base", align_bytes=64)
        nc.sync.dma_start(out=base_sb[:], in_=base)
        quantize(dg_op)
        product(ta_ps[:], dg_op, 0, kw[:], k_plane[:])

        def per_row(name, tag=None):
            return sb.tile([P, 1], F32, name=name, tag=tag or name, align_bytes=64)

        def per_slot(name, tag=None):
            return sb.tile([P, SLOTS], F32, name=name, tag=tag or name, align_bytes=64)

        rest, a2_sum, z = per_row("rest"), per_row("a2_sum", "a2_sum_then_ta"), per_row("z", "z_then_tz")
        a2 = per_slot("a2")
        nc.gpsimd.tensor_scalar(out=rest[:], in0=floor_sb[:], scalar1=float(SLOTS), scalar2=reserve_sb[:], op0=MULT, op1=ADD)
        nc.scalar.activation(out=a2[:], in_=a_ps[:], func=ACT.Square, accum_out=a2_sum[:])
        nc.scalar.activation(out=z[:], in_=a2_sum[:], func=ACT.Identity, bias=rest[:])
        ta = per_slot("ta", "a2_sum_then_ta")
        nc.scalar.activation(out=ta[:], in_=ta_ps[:], func=ACT.Copy, scale=GAIN)

        c = per_slot("c")
        banks = []
        for h in range(2):
            cols = slice(h * HALF, (h + 1) * HALF)
            c0_ps = ps.tile([P, HALF], F32, name="c0_ps%d" % h)
            vw = sb.tile([P, HALF], U16, name="vw%d" % h, align_bytes=64)
            nc.vector.tensor_copy(vw[:], v_words[:].indirect(half_of_list(h)))
            product(c0_ps[:], dg_op, Q, vw[:], v_plane[:, cols])
            banks.append((cols, c0_ps))
        r = per_row("r", "v_words_then_r")
        nc.vector.reciprocal(out=r[:], in_=z[:])
        for cols, c0_ps in banks:
            nc.scalar.activation(out=c[:, cols], in_=c0_ps[:], func=ACT.Identity, scale=r[:])

        neg_tz, slope, slope_m2 = per_row("neg_tz", "z_then_tz"), per_row("slope"), per_row("slope_m2")
        pc_sum, e, f, g = per_row("pc_sum"), per_row("e"), per_row("f"), per_row("g")
        neg_tp, pc, f_terms = per_slot("neg_tp"), per_slot("pc"), per_slot("f_terms")
        slope_c, a_part, ta_part = per_slot("slope_c"), per_slot("a_part"), per_slot("ta_part")
        nc.vector.scalar_tensor_tensor(
            out=neg_tp[:], in0=a_ps[:], scalar=-2.0, in1=ta[:], op0=MULT, op1=MULT, accum_out=neg_tz[:]
        )
        nc.scalar.activation(out=slope[:], in_=neg_tz[:], func=ACT.Identity, scale=r[:])
        nc.scalar.activation(out=slope_m2[:], in_=slope[:], func=ACT.Copy, scale=-2.0)
        nc.vector.scalar_tensor_tensor(
            out=pc[:], in0=a2[:], scalar=floor_sb[:], in1=c[:], op0=ADD, op1=MULT, accum_out=pc_sum[:]
        )
        nc.scalar.activation(out=e[:], in_=pc_sum[:], func=ACT.Identity, scale=r[:])
        nc.scalar.activation(out=slope_c[:], in_=c[:], func=ACT.Identity, scale=slope[:])
        nc.vector.scalar_tensor_tensor(
            out=f_terms[:], in0=c[:], scalar=r[:], in1=neg_tp[:], op0=MULT, op1=MULT, accum_out=f[:]
        )
        nc.scalar.activation(out=g[:], in_=e[:], func=ACT.Identity, scale=slope_m2[:], bias=f[:])
        nc.vector.scalar_tensor_tensor(out=ta_part[:], in0=c[:], scalar=e[:], in1=ta[:], op0=SUB, op1=MULT)
        nc.vector.scalar_tensor_tensor(out=a_part[:], in0=slope_c[:], scalar=g[:], in1=a_ps[:], op0=ADD, op1=MULT)
        nc.vector.tensor_tensor(window[:].indirect(offsets[:]), a_part[:], ta_part[:], ADD)

        start = 0
        for j, width in enumerate(STORE_WIDTHS):
            cols = slice(start, start + width)
            res = sb.tile([P, width], F32, name="res%d" % j, align_bytes=64)
            nc.vector.tensor_tensor(res[:], window[:, cols], base_sb[:, cols], ADD)
            (nc.sync if j % 2 == 0 else nc.scalar).dma_start(out=out[:, cols], in_=res[:])
            start += width
